import numpy as np
import ml_dtypes


def mxq(x, axis, fmt="e4m3"):
    dtype, down = {"e4m3": (ml_dtypes.float8_e4m3fn, 7), "e5m2": (ml_dtypes.float8_e5m2, 14)}[fmt]
    v = np.moveaxis(np.asarray(x, np.float32).astype(ml_dtypes.bfloat16).astype(np.float64), axis, -1)
    blocks = v.reshape(v.shape[:-1] + (-1, 32))
    amax = np.abs(blocks).max(-1, keepdims=True)
    byte = np.maximum(np.where(amax > 0, np.frexp(amax)[1] - 1 + 127, 0) - down, 1)
    scale = np.exp2(byte - 127.0)
    codes = (blocks / scale).astype(np.float32).astype(dtype).astype(np.float64)
    return np.moveaxis((codes * scale).reshape(v.shape), -1, axis)


WIDE = False


def mx_kscale(k):
    if not WIDE:
        return np.ones(k)
    levels = np.array([30, -30])
    if k % 512:
        return np.exp2(np.random.permutation(np.resize(levels, k // 32))).repeat(32)
    a = np.empty((k // 512, 16))
    for p in range(k // 512):
        a[p, :8] = np.random.permutation(np.resize(levels, 8))
        for g in range(8):
            far = levels[np.abs(levels - a[p, g]) >= 10]
            a[p, g + 8] = far[np.random.randint(len(far))]
    return np.exp2(a.ravel()).repeat(32)


def f64(x):
    return np.asarray(x).astype(np.float64)


def striped(idx):
    return np.tile(np.asarray(idx).reshape(-1, 16).T, (8, 1)).astype(np.uint16)


def unstriped(offs):
    return offs[:16].T.reshape(-1).astype(np.int64)


E2M1 = np.array([0.0, 0.5, 1.0, 1.5, 2.0, 3.0, 4.0, 6.0, -0.0, -0.5, -1.0, -1.5, -2.0, -3.0, -4.0, -6.0])


def pack_weight(w, fmt):
    k, n = w.shape
    w = f64(np.asarray(w, np.float32).astype(ml_dtypes.bfloat16)).reshape(k // 32, 32, n)
    amax = np.abs(w).max(1)
    if fmt in ("e4m3", "e5m2"):
        byte = np.frexp(amax)[1] - 1 + 127 - (7 if fmt == "e4m3" else 14)
    else:
        mant, ex = np.frexp(amax / 6.0)
        byte = np.where(mant > 0.5, ex, ex - 1) + 127
    byte = np.clip(np.where(amax > 0, byte, 1), 1, 254)
    scaled = (w * np.exp2(127.0 - byte)[:, None, :]).reshape(k, n).astype(np.float32)
    by_word = np.ascontiguousarray(scaled.reshape(k // 512, 128, 4, n).transpose(0, 1, 3, 2))
    if fmt in ("e4m3", "e5m2"):
        words = by_word.astype(ml_dtypes.float8_e4m3fn if fmt == "e4m3" else ml_dtypes.float8_e5m2).view(np.uint8)
    else:
        c = by_word.astype(ml_dtypes.float4_e2m1fn).view(np.uint8) & 0xF
        words = (c[..., 0::2] | (c[..., 1::2] << 4)).reshape(k // 512, 128, 2 * n)
    return np.ascontiguousarray(words), np.ascontiguousarray(byte.astype(np.uint8).reshape(k // 512, 16, n))


def unpack_weight(words, scales, fmt):
    g, _, n = scales.shape
    words = np.ascontiguousarray(words).reshape(g, 128, n, -1)
    if fmt in ("e4m3", "e5m2"):
        vals = words.view(ml_dtypes.float8_e4m3fn if fmt == "e4m3" else ml_dtypes.float8_e5m2).astype(np.float64)
    else:
        nib = np.empty((g, 128, n, 4), np.uint8)
        nib[..., 0::2] = words & 0xF
        nib[..., 1::2] = words >> 4
        vals = E2M1[nib]
    vals = vals * np.repeat(np.exp2(scales.astype(np.float64) - 127.0), 8, axis=1)[..., None]
    return vals.transpose(0, 1, 3, 2).reshape(g * 512, n)


K, T, J, R, F, Z, I, O, N, L, E = 512, 1024, 256, 512, 512, 1024, 256, 128, 256, 512, 512


def setup_inputs():
    n = np.random.standard_normal
    idx = np.random.permutation(T)[:J]
    idx2 = np.random.permutation(Z)[:J]
    idx3 = np.random.permutation(J)[:I]
    idx4 = np.random.permutation(J)[:O]
    idx5 = np.random.permutation(E)[:O]
    idx6 = np.random.permutation(E)[:O]
    ff = mx_kscale(F)
    fk = mx_kscale(K)
    fr = mx_kscale(R)
    fl = mx_kscale(L)
    xop = pack_weight(n((F, Z)) / ff[:, None], "e2m1")
    wp = pack_weight(n((K, R)) * 1 / np.sqrt(K) / fk[:, None] * fr, "e2m1")
    w2p = pack_weight(n((F, R)) * 1 / np.sqrt(F) * ff[:, None], "e5m2")
    wbp = pack_weight(n((R, N)) * 1 / np.sqrt(R) / fr[:, None], "e5m2")
    sxp = pack_weight(n((L, O)) / fl[:, None], "e2m1")
    wsp = pack_weight(n((L, N)) * 1 / np.sqrt(L) * fl[:, None], "e5m2")
    return {
        "xo_words": xop[0],
        "xo_scales": xop[1],
        "cq": (np.random.randint(-7, 8, (K, T)).astype(np.float64)).astype(np.float32),
        "gs": (np.random.uniform(0.1, 0.4, (K, 1)) * fk[:, None]).astype(np.float32),
        "w_words": wp[0],
        "w_scales": wp[1],
        "w2_words": w2p[0],
        "w2_scales": w2p[1],
        "wb_words": wbp[0],
        "wb_scales": wbp[1],
        "sx_words": sxp[0],
        "sx_scales": sxp[1],
        "ws_words": wsp[0],
        "ws_scales": wsp[1],
        "offs": striped(idx),
        "offs2": striped(idx2),
        "offs3": striped(idx3),
        "offs4": striped(idx4),
        "offs5": striped(idx5),
        "offs6": striped(idx6),
    }


def reference(xo_words, xo_scales, cq, gs, w_words, w_scales, w2_words, w2_scales, wb_words, wb_scales, sx_words, sx_scales, ws_words, ws_scales, offs, offs2, offs3, offs4, offs5, offs6):
    idx = unstriped(offs)
    idx2 = unstriped(offs2)
    idx3 = unstriped(offs3)
    idx4 = unstriped(offs4)
    idx5 = unstriped(offs5)
    idx6 = unstriped(offs6)
    xou = unpack_weight(xo_words, xo_scales, "e2m1")
    wu = unpack_weight(w_words, w_scales, "e2m1")
    w2u = unpack_weight(w2_words, w2_scales, "e5m2")
    wbu = unpack_weight(wb_words, wb_scales, "e5m2")
    sxu = unpack_weight(sx_words, sx_scales, "e2m1")
    wsu = unpack_weight(ws_words, ws_scales, "e5m2")
    x1 = f64(cq)[:, idx] * f64(gs)
    x1q = mxq(x1, 0, "e4m3")
    a = wu.T @ x1q
    xoidx2g = xou[:, idx2]
    b = w2u.T @ xoidx2g
    lb = b[:, 0:1]
    la = a[:, 0:1]
    h1 = a[:, idx3] * lb
    h2 = h1.reshape(R, O, I // O).max(axis=2)
    hid = np.abs(h2 - b[:, idx4] * la)
    hidq = mxq(hid, 0, "e4m3")
    p = wbu.T @ hidq + wsu.T @ sxu
    pa = np.zeros((N, E))
    pa[:, idx5] = p
    pb = np.zeros((N, E))
    pb[:, idx6] = p
    y = pa + pb
    return y

@@ -1,0 +1,177 @@
+from contextlib import ExitStack
+
+import concourse.mybir as mybir
+
+K, T, J, R, F, Z, I, O, N, L, E = 512, 1024, 256, 512, 512, 1024, 256, 128, 256, 512, 512
+FLOPS = 2 * (K * R * J + F * R * J + R * N * O + L * N * O)
+
+F32 = mybir.dt.float32
+BF16 = mybir.dt.bfloat16
+I32 = mybir.dt.int32
+U32 = mybir.dt.uint32
+U16 = mybir.dt.uint16
+U8 = mybir.dt.uint8
+E4M3 = mybir.dt.float8_e4m3fn_x4
+E5M2 = mybir.dt.float8_e5m2_x4
+E2M1 = mybir.dt.float4_e2m1fn_x4
+ALU = mybir.AluOpType
+ACT = mybir.ActivationFunctionType
+
+P = 128
+PACK = 4
+QUADS = 4
+QROWS = 4
+
+
+def tile_list_leadpool_codednote_further_pagetwice_kernel(
+    tc, xo_words, xo_scales, cq, gs, w_words, w_scales, w2_words, w2_scales, wb_words, wb_scales,
+    sx_words, sx_scales, ws_words, ws_scales, offs, offs2, offs3, offs4, offs5, offs6, out,
+):
+    nc = tc.nc
+    with ExitStack() as ctx:
+        lists = ctx.enter_context(tc.tile_pool(name="lists", bufs=1))
+        sb = ctx.enter_context(tc.tile_pool(name="sb", bufs=1))
+        psum = ctx.enter_context(tc.psum_pool(name="psum", bufs=1))
+
+        def tile(shape, dtype, name):
+            return sb.tile(shape, dtype, name=name, align_bytes=64)
+
+        def load_list(src, name):
+            t = lists.tile([P, src.shape[1]], U16, name=name)
+            nc.sync.dma_start(t[:], src)
+            return t
+
+        def staged_rows(src):
+            return src[0].bitcast(I32).rearrange("(q r) c -> r q c", r=QROWS)
+
+        xo_plane = tile([P, Z], U8, "xo_plane")
+        nc.gpsimd.memset(xo_plane[:].bitcast(I32), 0)
+        step = tile([P, PACK], F32, "step")
+        nc.gpsimd.dma_start(step[:], gs.rearrange("(p t) o -> p (t o)", t=PACK))
+        ww_plane = tile([P, 2 * R], U8, "ww_plane")
+        nc.vector.memset(ww_plane[:].bitcast(I32), 0)
+        wb_plane = tile([P, N], U8, "wb_plane")
+        ws_plane = tile([P, N], U8, "ws_plane")
+        sx_plane = tile([P, O], U8, "sx_plane")
+        for plane in (wb_plane, ws_plane, sx_plane):
+            nc.vector.memset(plane[:].bitcast(I32), 0)
+        a_rows = [tile([P, 2 * J], F32, "a_rows%d" % t) for t in range(PACK)]
+        for t in range(PACK):
+            nc.vector.memset(a_rows[t][:, J:], 0.0)
+        pages = [[tile([P, E], F32, "page%d_%d" % (u, h)) for h in range(N // P)] for u in range(2)]
+        for u in range(2):
+            for h in range(N // P):
+                (nc.vector if u == 0 else nc.gpsimd).memset(pages[u][h][:], 0.0)
+
+        cq_v = cq.rearrange("(p t) c -> p t c", t=PACK)
+        cq_rows = [tile([P, T], F32, "cq_rows%d" % t) for t in range(PACK)]
+        idx = load_list(offs, "idx")
+        nc.sync.dma_start(cq_rows[0][:], cq_v[:, 0, :])
+        nc.sync.dma_start(cq_rows[1][:], cq_v[:, 1, :])
+        ww_stage = tile([QROWS, QUADS, 2 * R // 4], I32, "ww_stage")
+        nc.scalar.dma_start(ww_stage[:, :, R // 4:], staged_rows(w2_scales))
+        nc.scalar.dma_start(ww_stage[:, :, :R // 4], staged_rows(w_scales))
+        for q in range(QUADS):
+            nc.scalar.dma_start(xo_plane[32 * q:32 * q + QROWS, :].bitcast(I32),
+                                xo_scales[0].bitcast(I32)[QROWS * q:QROWS * (q + 1), :])
+        idx2 = load_list(offs2, "idx2")
+        xo_w = tile([P, Z], U16, "xo_w")
+        nc.sync.dma_start(xo_w[:].bitcast(I32), xo_words[0].bitcast(I32))
+        w2_raw = tile([P, R], U32, "w2_raw")
+        nc.sync.dma_start(w2_raw[:].bitcast(I32), w2_words[0].rearrange("p n t -> p (n t)").bitcast(I32))
+        for t in range(2, PACK):
+            nc.sync.dma_start(cq_rows[t][:], cq_v[:, t, :])
+        w_raw = tile([P, R], U16, "w_raw")
+        nc.sync.dma_start(w_raw[:].bitcast(I32), w_words[0].bitcast(I32))
+        idx3 = load_list(offs3, "idx3")
+        idx4 = load_list(offs4, "idx4")
+        ws_w = tile([P, N], U32, "ws_w")
+        nc.sync.dma_start(ws_w[:].bitcast(I32), ws_words[0].rearrange("p n t -> p (n t)").bitcast(I32))
+        sx_w = tile([P, O], U16, "sx_w")
+        nc.sync.dma_start(sx_w[:].bitcast(I32), sx_words[0].bitcast(I32))
+        wb_w = tile([P, N], U32, "wb_w")
+        nc.sync.dma_start(wb_w[:].bitcast(I32), wb_words[0].rearrange("p n t -> p (n t)").bitcast(I32))
+        for plane, src in ((ws_plane, ws_scales), (sx_plane, sx_scales), (wb_plane, wb_scales)):
+            for q in range(QUADS):
+                nc.sync.dma_start(plane[32 * q:32 * q + QROWS, :].bitcast(I32),
+                                  src[0].bitcast(I32)[QROWS * q:QROWS * (q + 1), :])
+        idx5 = load_list(offs5, "idx5")
+        idx6 = load_list(offs6, "idx6")
+
+        for q in range(QUADS):
+            nc.vector.tensor_copy(ww_plane[32 * q:32 * q + QROWS, :].bitcast(I32), ww_stage[:, q, :])
+        ww_dealt = tile([P, 2, PACK, P], U8, "ww_dealt")
+        nc.vector.tensor_copy(ww_dealt[:], ww_plane[:].rearrange("p (u m t) -> p u t m", u=2, t=PACK))
+        xo_gs = tile([P, J], U8, "xo_gs")
+        nc.vector.tensor_copy(xo_gs[:], xo_plane[:].indirect(idx2[:]))
+        xo_g = tile([P, J], U16, "xo_g")
+        nc.vector.tensor_copy(xo_g[:], xo_w[:].indirect(idx2[:]))
+        w2_dealt = tile([P, PACK, P], U32, "w2_dealt")
+        nc.scalar.copy(w2_dealt[:], w2_raw[:].rearrange("p (m t) -> p t m", t=PACK))
+
+        b_banks = [psum.tile([P, 2, J], F32, name="b_bank%d" % u) for u in range(2)]
+        b_rows = [tile([P, J], F32, "b_rows%d" % t) for t in range(PACK)]
+        for t in range(PACK):
+            nc.tensor.matmul_mx(b_banks[t // 2][:, t % 2, :], lhsT=w2_dealt[:, t, :].bitcast(E5M2),
+                                lhsT_scale=ww_dealt[:, 1, t, :], rhs=xo_g[:].bitcast(E2M1), rhs_scale=xo_gs[:],
+                                start=True, stop=True)
+        for t in range(PACK):
+            nc.vector.tensor_copy(b_rows[t][:], b_banks[t // 2][:, t % 2, :])
+
+        x1_planes = tile([P, PACK, J], BF16, "x1_planes")
+        for t in range(PACK):
+            nc.scalar.activation(x1_planes[:, t, :], cq_rows[t][:].indirect(idx[:]), ACT.Copy, scale=step[:, t:t + 1])
+        w_dealt = tile([P, PACK, P], U16, "w_dealt")
+        nc.vector.tensor_copy(w_dealt[:], w_raw[:].rearrange("p (m t) -> p t m", t=PACK))
+        x1_woven = tile([P, J, PACK], BF16, "x1_woven")
+        halves = [slice(u * J // 2, (u + 1) * J // 2) for u in range(2)]
+        for cols in halves:
+            nc.vector.tensor_copy(x1_woven[:, cols, :].rearrange("p (c i) t -> p c t i", i=4),
+                                  x1_planes[:, :, cols].rearrange("p t (c i) -> p c t i", i=4))
+        x1_codes = tile([P, J], U32, "x1_codes")
+        x1_plane = tile([P, J], U8, "x1_plane")
+        for cols in halves:
+            nc.vector.quantize_mx(x1_codes[:, cols].bitcast(E4M3), x1_plane[:, cols],
+                                  x1_woven[:, cols, :].rearrange("p c t -> p (c t)"))
+
+        for t in range(PACK):
+            a_bank = psum.tile([P, J], F32, name="a_bank%d" % t)
+            nc.tensor.matmul_mx(a_bank[:], lhsT=w_dealt[:, t, :].bitcast(E2M1), lhsT_scale=ww_dealt[:, 0, t, :],
+                                rhs=x1_codes[:].bitcast(E4M3), rhs_scale=x1_plane[:], start=True, stop=True)
+            nc.vector.tensor_copy(a_rows[t][:, :J], a_bank[:])
+
+        p_banks = [psum.tile([P, O], F32, name="p_bank%d" % h) for h in range(N // P)]
+        for h in range(N // P):
+            cols = slice(h * P, (h + 1) * P)
+            nc.tensor.matmul_mx(p_banks[h][:], lhsT=ws_w[:, cols].bitcast(E5M2), lhsT_scale=ws_plane[:, cols],
+                                rhs=sx_w[:].bitcast(E2M1), rhs_scale=sx_plane[:], start=True, stop=False)
+
+        hid_woven = tile([P, O, PACK], BF16, "hid_woven")
+        for t in range(PACK):
+            picks = tile([P, I], F32, "picks%d" % t)
+            nc.scalar.activation(picks[:], a_rows[t][:].indirect(idx3[:]), ACT.Copy, scale=b_rows[t][:, 0:1])
+            beside = tile([P, O], F32, "beside%d" % t)
+            nc.scalar.activation(beside[:], b_rows[t][:].indirect(idx4[:]), ACT.Copy, scale=a_rows[t][:, 0:1])
+            pools = tile([P, O], F32, "pools%d" % t)
+            nc.vector.tensor_tensor(pools[:], picks[:, 0::2], picks[:, 1::2], ALU.max)
+            diff = tile([P, O], F32, "diff%d" % t)
+            nc.vector.tensor_tensor(diff[:], pools[:], beside[:], ALU.subtract)
+            nc.vector.scalar_tensor_tensor(hid_woven[:, :, t], diff[:], -1.0, diff[:], ALU.mult, ALU.max)
+        hid_codes = tile([P, O], U32, "hid_codes")
+        hid_plane = tile([P, O], U8, "hid_plane")
+        nc.vector.quantize_mx(hid_codes[:].bitcast(E4M3), hid_plane[:], hid_woven[:].rearrange("p c t -> p (c t)"))
+
+        p_rows = [tile([P, O], F32, "p_rows%d" % h) for h in range(N // P)]
+        for h in range(N // P):
+            cols = slice(h * P, (h + 1) * P)
+            nc.tensor.matmul_mx(p_banks[h][:], lhsT=wb_w[:, cols].bitcast(E5M2), lhsT_scale=wb_plane[:, cols],
+                                rhs=hid_codes[:].bitcast(E4M3), rhs_scale=hid_plane[:], start=False, stop=True)
+        nc.vector.tensor_copy(p_rows[0][:], p_banks[0][:])
+        nc.scalar.copy(p_rows[1][:], p_banks[1][:])
+        for h in range(N // P):
+            nc.vector.tensor_copy(pages[0][h][:].indirect(idx5[:]), p_rows[h][:])
+            nc.scalar.activation(pages[1][h][:].indirect(idx6[:]), p_rows[h][:], ACT.Copy)
+        for h, lo, hi, queue in ((0, 0, E, nc.sync), (1, 0, E // 2, nc.scalar), (1, E // 2, E, nc.sync)):
+            total = tile([P, hi - lo], F32, "total%d_%d" % (h, lo))
+            nc.vector.tensor_tensor(total[:], pages[0][h][:, lo:hi], pages[1][h][:, lo:hi], ALU.add)
+            queue.dma_start(out[h * P:(h + 1) * P, lo:hi], total[:])

@@ -45,9 +45,7 @@ def tile_list_leadpool_codednote_further_pagetwice_kernel(
             return src[0].bitcast(I32).rearrange("(q r) c -> r q c", r=QROWS)
 
         xo_plane = tile([P, Z], U8, "xo_plane")
-        nc.gpsimd.memset(xo_plane[:].bitcast(I32), 0)
-        step = tile([P, PACK], F32, "step")
-        nc.gpsimd.dma_start(step[:], gs.rearrange("(p t) o -> p (t o)", t=PACK))
+        nc.vector.memset(xo_plane[:].bitcast(I32), 0)
         ww_plane = tile([P, 2 * R], U8, "ww_plane")
         nc.vector.memset(ww_plane[:].bitcast(I32), 0)
         wb_plane = tile([P, N], U8, "wb_plane")
@@ -56,8 +54,9 @@ def tile_list_leadpool_codednote_further_pagetwice_kernel(
         for plane in (wb_plane, ws_plane, sx_plane):
             nc.vector.memset(plane[:].bitcast(I32), 0)
         a_rows = [tile([P, 2 * J], F32, "a_rows%d" % t) for t in range(PACK)]
-        for t in range(PACK):
-            nc.vector.memset(a_rows[t][:, J:], 0.0)
+        nc.gpsimd.memset(a_rows[0][:, J:], 0.0)
+        for t in range(1, PACK):
+            nc.scalar.activation(a_rows[t][:, J:], a_rows[0][:, J:], ACT.Copy)
         pages = [[tile([P, E], F32, "page%d_%d" % (u, h)) for h in range(N // P)] for u in range(2)]
         for u in range(2):
             for h in range(N // P):
@@ -65,22 +64,23 @@ def tile_list_leadpool_codednote_further_pagetwice_kernel(
 
         cq_v = cq.rearrange("(p t) c -> p t c", t=PACK)
         cq_rows = [tile([P, T], F32, "cq_rows%d" % t) for t in range(PACK)]
+        xo_stage = tile([QROWS, QUADS, Z // 4], I32, "xo_stage")
+        ww_stage = tile([QROWS, QUADS, 2 * R // 4], I32, "ww_stage")
+        nc.sync.dma_start(xo_stage[:], staged_rows(xo_scales))
+        step = tile([P, PACK], F32, "step")
+        nc.scalar.dma_start(step[:], gs.rearrange("(p t) o -> p (t o)", t=PACK))
+        nc.sync.dma_start(ww_stage[:, :, R // 4:], staged_rows(w2_scales))
+        nc.sync.dma_start(ww_stage[:, :, :R // 4], staged_rows(w_scales))
         idx = load_list(offs, "idx")
+        idx2 = load_list(offs2, "idx2")
         nc.sync.dma_start(cq_rows[0][:], cq_v[:, 0, :])
         nc.sync.dma_start(cq_rows[1][:], cq_v[:, 1, :])
-        ww_stage = tile([QROWS, QUADS, 2 * R // 4], I32, "ww_stage")
-        nc.scalar.dma_start(ww_stage[:, :, R // 4:], staged_rows(w2_scales))
-        nc.scalar.dma_start(ww_stage[:, :, :R // 4], staged_rows(w_scales))
-        for q in range(QUADS):
-            nc.scalar.dma_start(xo_plane[32 * q:32 * q + QROWS, :].bitcast(I32),
-                                xo_scales[0].bitcast(I32)[QROWS * q:QROWS * (q + 1), :])
-        idx2 = load_list(offs2, "idx2")
         xo_w = tile([P, Z], U16, "xo_w")
         nc.sync.dma_start(xo_w[:].bitcast(I32), xo_words[0].bitcast(I32))
-        w2_raw = tile([P, R], U32, "w2_raw")
-        nc.sync.dma_start(w2_raw[:].bitcast(I32), w2_words[0].rearrange("p n t -> p (n t)").bitcast(I32))
         for t in range(2, PACK):
             nc.sync.dma_start(cq_rows[t][:], cq_v[:, t, :])
+        w2_raw = sb.tile([P, R], U32, name="w2_raw", tag="w2_then_x1", align_bytes=64)
+        nc.sync.dma_start(w2_raw[:].bitcast(I32), w2_words[0].rearrange("p n t -> p (n t)").bitcast(I32))
         w_raw = tile([P, R], U16, "w_raw")
         nc.sync.dma_start(w_raw[:].bitcast(I32), w_words[0].bitcast(I32))
         idx3 = load_list(offs3, "idx3")
@@ -99,7 +99,8 @@ def tile_list_leadpool_codednote_further_pagetwice_kernel(
         idx6 = load_list(offs6, "idx6")
 
         for q in range(QUADS):
-            nc.vector.tensor_copy(ww_plane[32 * q:32 * q + QROWS, :].bitcast(I32), ww_stage[:, q, :])
+            for plane, stage in ((xo_plane, xo_stage), (ww_plane, ww_stage)):
+                nc.vector.tensor_copy(plane[32 * q:32 * q + QROWS, :].bitcast(I32), stage[:, q, :])
         ww_dealt = tile([P, 2, PACK, P], U8, "ww_dealt")
         nc.vector.tensor_copy(ww_dealt[:], ww_plane[:].rearrange("p (u m t) -> p u t m", u=2, t=PACK))
         xo_gs = tile([P, J], U8, "xo_gs")
@@ -107,23 +108,23 @@ def tile_list_leadpool_codednote_further_pagetwice_kernel(
         xo_g = tile([P, J], U16, "xo_g")
         nc.vector.tensor_copy(xo_g[:], xo_w[:].indirect(idx2[:]))
         w2_dealt = tile([P, PACK, P], U32, "w2_dealt")
-        nc.scalar.copy(w2_dealt[:], w2_raw[:].rearrange("p (m t) -> p t m", t=PACK))
+        nc.vector.tensor_copy(w2_dealt[:], w2_raw[:].rearrange("p (m t) -> p t m", t=PACK))
 
-        b_banks = [psum.tile([P, 2, J], F32, name="b_bank%d" % u) for u in range(2)]
+        b_banks = [psum.tile([P, J], F32, name="b_bank%d" % t) for t in range(PACK)]
         b_rows = [tile([P, J], F32, "b_rows%d" % t) for t in range(PACK)]
         for t in range(PACK):
-            nc.tensor.matmul_mx(b_banks[t // 2][:, t % 2, :], lhsT=w2_dealt[:, t, :].bitcast(E5M2),
+            nc.tensor.matmul_mx(b_banks[t][:], lhsT=w2_dealt[:, t, :].bitcast(E5M2),
                                 lhsT_scale=ww_dealt[:, 1, t, :], rhs=xo_g[:].bitcast(E2M1), rhs_scale=xo_gs[:],
                                 start=True, stop=True)
-        for t in range(PACK):
-            nc.vector.tensor_copy(b_rows[t][:], b_banks[t // 2][:, t % 2, :])
 
         x1_planes = tile([P, PACK, J], BF16, "x1_planes")
         for t in range(PACK):
             nc.scalar.activation(x1_planes[:, t, :], cq_rows[t][:].indirect(idx[:]), ACT.Copy, scale=step[:, t:t + 1])
         w_dealt = tile([P, PACK, P], U16, "w_dealt")
-        nc.vector.tensor_copy(w_dealt[:], w_raw[:].rearrange("p (m t) -> p t m", t=PACK))
-        x1_woven = tile([P, J, PACK], BF16, "x1_woven")
+        nc.scalar.copy(w_dealt[:], w_raw[:].rearrange("p (m t) -> p t m", t=PACK))
+        for t in range(PACK):
+            nc.scalar.copy(b_rows[t][:], b_banks[t][:])
+        x1_woven = sb.tile([P, J, PACK], BF16, name="x1_woven", tag="w2_then_x1", align_bytes=64)
         halves = [slice(u * J // 2, (u + 1) * J // 2) for u in range(2)]
         for cols in halves:
             nc.vector.tensor_copy(x1_woven[:, cols, :].rearrange("p (c i) t -> p c t i", i=4),
@@ -135,12 +136,12 @@ def tile_list_leadpool_codednote_further_pagetwice_kernel(
                                   x1_woven[:, cols, :].rearrange("p c t -> p (c t)"))
 
         for t in range(PACK):
-            a_bank = psum.tile([P, J], F32, name="a_bank%d" % t)
+            a_bank = psum.tile([P, J], F32, name="a_bank%d" % t, tag="bank%d" % t)
             nc.tensor.matmul_mx(a_bank[:], lhsT=w_dealt[:, t, :].bitcast(E2M1), lhsT_scale=ww_dealt[:, 0, t, :],
                                 rhs=x1_codes[:].bitcast(E4M3), rhs_scale=x1_plane[:], start=True, stop=True)
             nc.vector.tensor_copy(a_rows[t][:, :J], a_bank[:])
 
-        p_banks = [psum.tile([P, O], F32, name="p_bank%d" % h) for h in range(N // P)]
+        p_banks = [psum.tile([P, O], F32, name="p_bank%d" % h, tag="bank%d" % h) for h in range(N // P)]
         for h in range(N // P):
             cols = slice(h * P, (h + 1) * P)
             nc.tensor.matmul_mx(p_banks[h][:], lhsT=ws_w[:, cols].bitcast(E5M2), lhsT_scale=ws_plane[:, cols],

@@ -77,10 +77,10 @@ def tile_list_leadpool_codednote_further_pagetwice_kernel(
         nc.sync.dma_start(cq_rows[1][:], cq_v[:, 1, :])
         xo_w = tile([P, Z], U16, "xo_w")
         nc.sync.dma_start(xo_w[:].bitcast(I32), xo_words[0].bitcast(I32))
+        w2_raw = tile([P, R], U32, "w2_raw")
+        nc.sync.dma_start(w2_raw[:].bitcast(I32), w2_words[0].rearrange("p n t -> p (n t)").bitcast(I32))
         for t in range(2, PACK):
             nc.sync.dma_start(cq_rows[t][:], cq_v[:, t, :])
-        w2_raw = sb.tile([P, R], U32, name="w2_raw", tag="w2_then_x1", align_bytes=64)
-        nc.sync.dma_start(w2_raw[:].bitcast(I32), w2_words[0].rearrange("p n t -> p (n t)").bitcast(I32))
         w_raw = tile([P, R], U16, "w_raw")
         nc.sync.dma_start(w_raw[:].bitcast(I32), w_words[0].bitcast(I32))
         idx3 = load_list(offs3, "idx3")
@@ -102,29 +102,30 @@ def tile_list_leadpool_codednote_further_pagetwice_kernel(
             for plane, stage in ((xo_plane, xo_stage), (ww_plane, ww_stage)):
                 nc.vector.tensor_copy(plane[32 * q:32 * q + QROWS, :].bitcast(I32), stage[:, q, :])
         ww_dealt = tile([P, 2, PACK, P], U8, "ww_dealt")
-        nc.vector.tensor_copy(ww_dealt[:], ww_plane[:].rearrange("p (u m t) -> p u t m", u=2, t=PACK))
+        ww_dealing = ww_plane[:].rearrange("p (u m t) -> p u t m", u=2, t=PACK)
+        nc.vector.tensor_copy(ww_dealt[:, 1], ww_dealing[:, 1])
         xo_gs = tile([P, J], U8, "xo_gs")
         nc.vector.tensor_copy(xo_gs[:], xo_plane[:].indirect(idx2[:]))
         xo_g = tile([P, J], U16, "xo_g")
         nc.vector.tensor_copy(xo_g[:], xo_w[:].indirect(idx2[:]))
         w2_dealt = tile([P, PACK, P], U32, "w2_dealt")
-        nc.vector.tensor_copy(w2_dealt[:], w2_raw[:].rearrange("p (m t) -> p t m", t=PACK))
+        nc.scalar.copy(w2_dealt[:], w2_raw[:].rearrange("p (m t) -> p t m", t=PACK))
+        nc.vector.tensor_copy(ww_dealt[:, 0], ww_dealing[:, 0])
 
-        b_banks = [psum.tile([P, J], F32, name="b_bank%d" % t) for t in range(PACK)]
+        b_banks = [psum.tile([P, J], F32, name="b_bank%d" % t, tag="bank%d" % (PACK + t)) for t in range(PACK)]
         b_rows = [tile([P, J], F32, "b_rows%d" % t) for t in range(PACK)]
         for t in range(PACK):
             nc.tensor.matmul_mx(b_banks[t][:], lhsT=w2_dealt[:, t, :].bitcast(E5M2),
                                 lhsT_scale=ww_dealt[:, 1, t, :], rhs=xo_g[:].bitcast(E2M1), rhs_scale=xo_gs[:],
                                 start=True, stop=True)
+            nc.vector.tensor_copy(b_rows[t][:], b_banks[t][:])
 
         x1_planes = tile([P, PACK, J], BF16, "x1_planes")
         for t in range(PACK):
             nc.scalar.activation(x1_planes[:, t, :], cq_rows[t][:].indirect(idx[:]), ACT.Copy, scale=step[:, t:t + 1])
         w_dealt = tile([P, PACK, P], U16, "w_dealt")
         nc.scalar.copy(w_dealt[:], w_raw[:].rearrange("p (m t) -> p t m", t=PACK))
-        for t in range(PACK):
-            nc.scalar.copy(b_rows[t][:], b_banks[t][:])
-        x1_woven = sb.tile([P, J, PACK], BF16, name="x1_woven", tag="w2_then_x1", align_bytes=64)
+        x1_woven = tile([P, J, PACK], BF16, "x1_woven")
         halves = [slice(u * J // 2, (u + 1) * J // 2) for u in range(2)]
         for cols in halves:
             nc.vector.tensor_copy(x1_woven[:, cols, :].rearrange("p (c i) t -> p c t i", i=4),
@@ -135,29 +136,47 @@ def tile_list_leadpool_codednote_further_pagetwice_kernel(
             nc.vector.quantize_mx(x1_codes[:, cols].bitcast(E4M3), x1_plane[:, cols],
                                   x1_woven[:, cols, :].rearrange("p c t -> p (c t)"))
 
-        for t in range(PACK):
-            a_bank = psum.tile([P, J], F32, name="a_bank%d" % t, tag="bank%d" % t)
-            nc.tensor.matmul_mx(a_bank[:], lhsT=w_dealt[:, t, :].bitcast(E2M1), lhsT_scale=ww_dealt[:, 0, t, :],
-                                rhs=x1_codes[:].bitcast(E4M3), rhs_scale=x1_plane[:], start=True, stop=True)
-            nc.vector.tensor_copy(a_rows[t][:, :J], a_bank[:])
+        for u, cols in enumerate(halves):
+            for t in range(PACK):
+                a_bank = psum.tile([P, J // 2], F32, name="a_bank%d_%d" % (u, t), tag="bank%d" % (PACK * u + t))
+                nc.tensor.matmul_mx(a_bank[:], lhsT=w_dealt[:, t, :].bitcast(E2M1), lhsT_scale=ww_dealt[:, 0, t, :],
+                                    rhs=x1_codes[:, cols].bitcast(E4M3), rhs_scale=x1_plane[:, cols], start=True, stop=True)
+                nc.vector.tensor_copy(a_rows[t][:, cols], a_bank[:])
 
-        p_banks = [psum.tile([P, O], F32, name="p_bank%d" % h, tag="bank%d" % h) for h in range(N // P)]
+        p_banks = [psum.tile([P, O], F32, name="p_bank%d" % h, tag="bank%d" % (PACK + h)) for h in range(N // P)]
         for h in range(N // P):
             cols = slice(h * P, (h + 1) * P)
             nc.tensor.matmul_mx(p_banks[h][:], lhsT=ws_w[:, cols].bitcast(E5M2), lhsT_scale=ws_plane[:, cols],
                                 rhs=sx_w[:].bitcast(E2M1), rhs_scale=sx_plane[:], start=True, stop=False)
 
         hid_woven = tile([P, O, PACK], BF16, "hid_woven")
+        diff = tile([P, PACK, O], F32, "diff")
+        last = PACK - 1
+
+        def look_beside(t, beside, lo, hi):
+            nc.scalar.activation(beside[:, lo:hi], b_rows[t][:].indirect(idx4[:, lo // 16:hi // 16]), ACT.Copy,
+                                 scale=a_rows[t][:, 0:1])
+
+        def subtract(t, pools, beside, lo, hi):
+            nc.vector.tensor_tensor(diff[:, t, lo:hi], pools[:, lo:hi], beside[:, lo:hi], ALU.subtract)
+            if t % 2 == 1:
+                pair = diff[:, t - 1:t + 1, lo:hi].rearrange("p t o -> p o t")
+                nc.vector.scalar_tensor_tensor(hid_woven[:, lo:hi, t - 1:t + 1], pair, -1.0, pair, ALU.mult, ALU.max)
+
+        besides = [tile([P, O], F32, "beside%d" % t) for t in range(last)]
+        for t in range(last):
+            look_beside(t, besides[t], 0, O)
         for t in range(PACK):
-            picks = tile([P, I], F32, "picks%d" % t)
+            picks = sb.tile([P, I], F32, name="picks%d" % t, tag="picks%d" % t, align_bytes=64)
             nc.scalar.activation(picks[:], a_rows[t][:].indirect(idx3[:]), ACT.Copy, scale=b_rows[t][:, 0:1])
-            beside = tile([P, O], F32, "beside%d" % t)
-            nc.scalar.activation(beside[:], b_rows[t][:].indirect(idx4[:]), ACT.Copy, scale=a_rows[t][:, 0:1])
             pools = tile([P, O], F32, "pools%d" % t)
             nc.vector.tensor_tensor(pools[:], picks[:, 0::2], picks[:, 1::2], ALU.max)
-            diff = tile([P, O], F32, "diff%d" % t)
-            nc.vector.tensor_tensor(diff[:], pools[:], beside[:], ALU.subtract)
-            nc.vector.scalar_tensor_tensor(hid_woven[:, :, t], diff[:], -1.0, diff[:], ALU.mult, ALU.max)
+            if t < last:
+                subtract(t, pools, besides[t], 0, O)
+        beside = sb.tile([P, O], F32, name="beside_last", tag="picks%d" % (last - 1), align_bytes=64)
+        for lo, hi in ((0, O // 2), (O // 2, O)):
+            look_beside(last, beside, lo, hi)
+            subtract(last, pools, beside, lo, hi)
         hid_codes = tile([P, O], U32, "hid_codes")
         hid_plane = tile([P, O], U8, "hid_plane")
         nc.vector.quantize_mx(hid_codes[:].bitcast(E4M3), hid_plane[:], hid_woven[:].rearrange("p c t -> p (c t)"))

from contextlib import ExitStack

import concourse.mybir as mybir

K, T, J, R, F, Z, I, O, N, L, E = 512, 1024, 256, 512, 512, 1024, 256, 128, 256, 512, 512
FLOPS = 2 * (K * R * J + F * R * J + R * N * O + L * N * O)

F32 = mybir.dt.float32
BF16 = mybir.dt.bfloat16
I32 = mybir.dt.int32
U32 = mybir.dt.uint32
U16 = mybir.dt.uint16
U8 = mybir.dt.uint8
E4M3 = mybir.dt.float8_e4m3fn_x4
E5M2 = mybir.dt.float8_e5m2_x4
E2M1 = mybir.dt.float4_e2m1fn_x4
ALU = mybir.AluOpType
ACT = mybir.ActivationFunctionType

P = 128
PACK = 4
QUADS = 4
QROWS = 4


def tile_list_leadpool_codednote_further_pagetwice_kernel(
    tc, xo_words, xo_scales, cq, gs, w_words, w_scales, w2_words, w2_scales, wb_words, wb_scales,
    sx_words, sx_scales, ws_words, ws_scales, offs, offs2, offs3, offs4, offs5, offs6, out,
):
    nc = tc.nc
    with ExitStack() as ctx:
        lists = ctx.enter_context(tc.tile_pool(name="lists", bufs=1))
        sb = ctx.enter_context(tc.tile_pool(name="sb", bufs=1))
        psum = ctx.enter_context(tc.psum_pool(name="psum", bufs=1))

        def tile(shape, dtype, name):
            return sb.tile(shape, dtype, name=name, align_bytes=64)

        def load_list(src, name):
            t = lists.tile([P, src.shape[1]], U16, name=name)
            nc.sync.dma_start(t[:], src)
            return t

        def staged_rows(src):
            return src[0].bitcast(I32).rearrange("(q r) c -> r q c", r=QROWS)

        xo_plane = tile([P, Z], U8, "xo_plane")
        nc.vector.memset(xo_plane[:].bitcast(I32), 0)
        ww_plane = tile([P, 2 * R], U8, "ww_plane")
        nc.vector.memset(ww_plane[:].bitcast(I32), 0)
        wb_plane = tile([P, N], U8, "wb_plane")
        ws_plane = tile([P, N], U8, "ws_plane")
        sx_plane = tile([P, O], U8, "sx_plane")
        for plane in (wb_plane, ws_plane, sx_plane):
            nc.vector.memset(plane[:].bitcast(I32), 0)
        a_rows = [tile([P, 2 * J], F32, "a_rows%d" % t) for t in range(PACK)]
        nc.gpsimd.memset(a_rows[0][:, J:], 0.0)
        for t in range(1, PACK):
            nc.scalar.activation(a_rows[t][:, J:], a_rows[0][:, J:], ACT.Copy)
        pages = [[tile([P, E], F32, "page%d_%d" % (u, h)) for h in range(N // P)] for u in range(2)]
        for u in range(2):
            for h in range(N // P):
                (nc.vector if u == 0 else nc.gpsimd).memset(pages[u][h][:], 0.0)

        cq_v = cq.rearrange("(p t) c -> p t c", t=PACK)
        cq_rows = [tile([P, T], F32, "cq_rows%d" % t) for t in range(PACK)]
        xo_stage = tile([QROWS, QUADS, Z // 4], I32, "xo_stage")
        ww_stage = tile([QROWS, QUADS, 2 * R // 4], I32, "ww_stage")
        nc.sync.dma_start(xo_stage[:], staged_rows(xo_scales))
        step = tile([P, PACK], F32, "step")
        nc.scalar.dma_start(step[:], gs.rearrange("(p t) o -> p (t o)", t=PACK))
        nc.sync.dma_start(ww_stage[:, :, R // 4:], staged_rows(w2_scales))
        nc.sync.dma_start(ww_stage[:, :, :R // 4], staged_rows(w_scales))
        idx = load_list(offs, "idx")
        idx2 = load_list(offs2, "idx2")
        nc.sync.dma_start(cq_rows[0][:], cq_v[:, 0, :])
        nc.sync.dma_start(cq_rows[1][:], cq_v[:, 1, :])
        xo_w = tile([P, Z], U16, "xo_w")
        nc.sync.dma_start(xo_w[:].bitcast(I32), xo_words[0].bitcast(I32))
        w2_raw = tile([P, R], U32, "w2_raw")
        nc.sync.dma_start(w2_raw[:].bitcast(I32), w2_words[0].rearrange("p n t -> p (n t)").bitcast(I32))
        for t in range(2, PACK):
            nc.sync.dma_start(cq_rows[t][:], cq_v[:, t, :])
        w_raw = tile([P, R], U16, "w_raw")
        nc.sync.dma_start(w_raw[:].bitcast(I32), w_words[0].bitcast(I32))
        idx3 = load_list(offs3, "idx3")
        idx4 = load_list(offs4, "idx4")
        ws_w = tile([P, N], U32, "ws_w")
        nc.sync.dma_start(ws_w[:].bitcast(I32), ws_words[0].rearrange("p n t -> p (n t)").bitcast(I32))
        sx_w = tile([P, O], U16, "sx_w")
        nc.sync.dma_start(sx_w[:].bitcast(I32), sx_words[0].bitcast(I32))
        wb_w = tile([P, N], U32, "wb_w")
        nc.sync.dma_start(wb_w[:].bitcast(I32), wb_words[0].rearrange("p n t -> p (n t)").bitcast(I32))
        for plane, src in ((ws_plane, ws_scales), (sx_plane, sx_scales), (wb_plane, wb_scales)):
            for q in range(QUADS):
                nc.sync.dma_start(plane[32 * q:32 * q + QROWS, :].bitcast(I32),
                                  src[0].bitcast(I32)[QROWS * q:QROWS * (q + 1), :])
        idx5 = load_list(offs5, "idx5")
        idx6 = load_list(offs6, "idx6")

        for q in range(QUADS):
            for plane, stage in ((xo_plane, xo_stage), (ww_plane, ww_stage)):
                nc.vector.tensor_copy(plane[32 * q:32 * q + QROWS, :].bitcast(I32), stage[:, q, :])
        ww_dealt = tile([P, 2, PACK, P], U8, "ww_dealt")
        ww_dealing = ww_plane[:].rearrange("p (u m t) -> p u t m", u=2, t=PACK)
        nc.vector.tensor_copy(ww_dealt[:, 1], ww_dealing[:, 1])
        xo_gs = tile([P, J], U8, "xo_gs")
        nc.vector.tensor_copy(xo_gs[:], xo_plane[:].indirect(idx2[:]))
        xo_g = tile([P, J], U16, "xo_g")
        nc.vector.tensor_copy(xo_g[:], xo_w[:].indirect(idx2[:]))
        w2_dealt = tile([P, PACK, P], U32, "w2_dealt")
        nc.scalar.copy(w2_dealt[:], w2_raw[:].rearrange("p (m t) -> p t m", t=PACK))
        nc.vector.tensor_copy(ww_dealt[:, 0], ww_dealing[:, 0])

        b_banks = [psum.tile([P, J], F32, name="b_bank%d" % t, tag="bank%d" % (PACK + t)) for t in range(PACK)]
        b_rows = [tile([P, J], F32, "b_rows%d" % t) for t in range(PACK)]
        for t in range(PACK):
            nc.tensor.matmul_mx(b_banks[t][:], lhsT=w2_dealt[:, t, :].bitcast(E5M2),
                                lhsT_scale=ww_dealt[:, 1, t, :], rhs=xo_g[:].bitcast(E2M1), rhs_scale=xo_gs[:],
                                start=True, stop=True)
            nc.vector.tensor_copy(b_rows[t][:], b_banks[t][:])

        x1_planes = tile([P, PACK, J], BF16, "x1_planes")
        for t in range(PACK):
            nc.scalar.activation(x1_planes[:, t, :], cq_rows[t][:].indirect(idx[:]), ACT.Copy, scale=step[:, t:t + 1])
        w_dealt = tile([P, PACK, P], U16, "w_dealt")
        nc.scalar.copy(w_dealt[:], w_raw[:].rearrange("p (m t) -> p t m", t=PACK))
        x1_woven = tile([P, J, PACK], BF16, "x1_woven")
        halves = [slice(u * J // 2, (u + 1) * J // 2) for u in range(2)]
        for cols in halves:
            nc.vector.tensor_copy(x1_woven[:, cols, :].rearrange("p (c i) t -> p c t i", i=4),
                                  x1_planes[:, :, cols].rearrange("p t (c i) -> p c t i", i=4))
        x1_codes = tile([P, J], U32, "x1_codes")
        x1_plane = tile([P, J], U8, "x1_plane")
        for cols in halves:
            nc.vector.quantize_mx(x1_codes[:, cols].bitcast(E4M3), x1_plane[:, cols],
                                  x1_woven[:, cols, :].rearrange("p c t -> p (c t)"))

        for u, cols in enumerate(halves):
            for t in range(PACK):
                a_bank = psum.tile([P, J // 2], F32, name="a_bank%d_%d" % (u, t), tag="bank%d" % (PACK * u + t))
                nc.tensor.matmul_mx(a_bank[:], lhsT=w_dealt[:, t, :].bitcast(E2M1), lhsT_scale=ww_dealt[:, 0, t, :],
                                    rhs=x1_codes[:, cols].bitcast(E4M3), rhs_scale=x1_plane[:, cols], start=True, stop=True)
                nc.vector.tensor_copy(a_rows[t][:, cols], a_bank[:])

        p_banks = [psum.tile([P, O], F32, name="p_bank%d" % h, tag="bank%d" % (PACK + h)) for h in range(N // P)]
        for h in range(N // P):
            cols = slice(h * P, (h + 1) * P)
            nc.tensor.matmul_mx(p_banks[h][:], lhsT=ws_w[:, cols].bitcast(E5M2), lhsT_scale=ws_plane[:, cols],
                                rhs=sx_w[:].bitcast(E2M1), rhs_scale=sx_plane[:], start=True, stop=False)

        hid_woven = tile([P, O, PACK], BF16, "hid_woven")
        diff = tile([P, PACK, O], F32, "diff")
        last = PACK - 1

        def look_beside(t, beside, lo, hi):
            nc.scalar.activation(beside[:, lo:hi], b_rows[t][:].indirect(idx4[:, lo // 16:hi // 16]), ACT.Copy,
                                 scale=a_rows[t][:, 0:1])

        def subtract(t, pools, beside, lo, hi):
            nc.vector.tensor_tensor(diff[:, t, lo:hi], pools[:, lo:hi], beside[:, lo:hi], ALU.subtract)
            if t % 2 == 1:
                pair = diff[:, t - 1:t + 1, lo:hi].rearrange("p t o -> p o t")
                nc.vector.scalar_tensor_tensor(hid_woven[:, lo:hi, t - 1:t + 1], pair, -1.0, pair, ALU.mult, ALU.max)

        besides = [tile([P, O], F32, "beside%d" % t) for t in range(last)]
        for t in range(last):
            look_beside(t, besides[t], 0, O)
        for t in range(PACK):
            picks = sb.tile([P, I], F32, name="picks%d" % t, tag="picks%d" % t, align_bytes=64)
            nc.scalar.activation(picks[:], a_rows[t][:].indirect(idx3[:]), ACT.Copy, scale=b_rows[t][:, 0:1])
            pools = tile([P, O], F32, "pools%d" % t)
            nc.vector.tensor_tensor(pools[:], picks[:, 0::2], picks[:, 1::2], ALU.max)
            if t < last:
                subtract(t, pools, besides[t], 0, O)
        beside = sb.tile([P, O], F32, name="beside_last", tag="picks%d" % (last - 1), align_bytes=64)
        for lo, hi in ((0, O // 2), (O // 2, O)):
            look_beside(last, beside, lo, hi)
            subtract(last, pools, beside, lo, hi)
        hid_codes = tile([P, O], U32, "hid_codes")
        hid_plane = tile([P, O], U8, "hid_plane")
        nc.vector.quantize_mx(hid_codes[:].bitcast(E4M3), hid_plane[:], hid_woven[:].rearrange("p c t -> p (c t)"))

        p_rows = [tile([P, O], F32, "p_rows%d" % h) for h in range(N // P)]
        for h in range(N // P):
            cols = slice(h * P, (h + 1) * P)
            nc.tensor.matmul_mx(p_banks[h][:], lhsT=wb_w[:, cols].bitcast(E5M2), lhsT_scale=wb_plane[:, cols],
                                rhs=hid_codes[:].bitcast(E4M3), rhs_scale=hid_plane[:], start=False, stop=True)
        nc.vector.tensor_copy(p_rows[0][:], p_banks[0][:])
        nc.scalar.copy(p_rows[1][:], p_banks[1][:])
        for h in range(N // P):
            nc.vector.tensor_copy(pages[0][h][:].indirect(idx5[:]), p_rows[h][:])
            nc.scalar.activation(pages[1][h][:].indirect(idx6[:]), p_rows[h][:], ACT.Copy)
        for h, lo, hi, queue in ((0, 0, E, nc.sync), (1, 0, E // 2, nc.scalar), (1, E // 2, E, nc.sync)):
            total = tile([P, hi - lo], F32, "total%d_%d" % (h, lo))
            nc.vector.tensor_tensor(total[:], pages[0][h][:, lo:hi], pages[1][h][:, lo:hi], ALU.add)
            queue.dma_start(out[h * P:(h + 1) * P, lo:hi], total[:])
